import numpy as np, ml_dtypes
CORES = [7,391,135,263,15,399,143,271]
N = 8
import mx_ref
NC, W = 128, 6
BF = ml_dtypes.bfloat16
def cut(t, i, w=512):
    return t[:, w * i:w * i + w]
def term(a, B):
    return np.stack([mx_ref.matmul(mx_ref.quantize(cut(a, i)), B) for i in range(4)], axis=2).reshape(128, -1)
def setup_inputs(rng):
    def f(*shape):
        return mx_ref.flush((rng.standard_normal(shape, dtype=np.float32) * np.exp2(rng.integers(-2, 3, shape[:-1] + (1,)))).astype(BF))
    return {"a": f(N, 128, 4 * 512), "b": f(N, 128, 4 * NC)}
def setup_inputs_blocks(rng):
    d = setup_inputs(rng)
    for k in ("a", "b"): d[k] = mx_ref.spread(d[k], rng, 2)
    return d
def setup_inputs_wide(rng):
    d = setup_inputs(rng)
    for k in ("a", "b"): d[k] = mx_ref.flush((d[k].astype(np.float32) * np.exp2(rng.integers(-4, 5, (N, 1, 1))).astype(np.float32)).astype(BF))
    return d
def setup_inputs_lossless(rng):
    a = np.zeros((N, 128, 4 * 128, 4), np.float32)
    for r in range(N):
        k = rng.integers(0, 512, size=4 * 128)
        a[r, k // 4, np.arange(4 * 128), k % 4] = 1.0
    size = np.repeat(2.0 ** rng.integers(-4, 5, size=(1, 1, (4 * NC) // 4)), 4, axis=2)
    b = rng.integers(-1, 2, size=(N, 128, 4 * NC)) * size
    return {"a": a.reshape(N, 128, 4 * 512).astype(BF), "b": b.astype(np.float32).astype(BF)}
def reference(a, b):
    T = [term(a[r], mx_ref.quantize(b[r])) for r in range(N)]
    y = np.zeros((N, 128, 4 * NC), np.float32)
    for c in range(N):
        y[c] = mx_ref.total([T[(c - k) % N] for k in range(W)])
    return {"y": y}

from concourse.mybir import AluOpType, ActivationFunctionType

C = 128
H = C // 2
F8, U8, BF, F32 = "float8_e4m3fn_x4", "uint8", "bfloat16", "float32"

SCRATCH = {
    "xa": ("sbuf", [128, 16 * C], BF), "xb": ("sbuf", [128, 4 * C], BF),
    "eye": ("sbuf", [128, 8 * C + 4], BF),
    "tt": ("sbuf", [128, 4 * C], BF), "pp": ("sbuf", [128, 4 * C], BF), "yt": ("sbuf", [128, 4 * C], F32),
    "qa": ("sbuf", [128, 4 * C], F8), "sa": ("sbuf", [128, 4 * C], U8),
    "qb": ("sbuf", [128, C], F8), "sb": ("sbuf", [128, C], U8),
    "qw": ("sbuf", [128, 4 * C], F8), "sw": ("sbuf", [128, 4 * C], U8),
    "qt": ("sbuf", [128, C], F8), "st": ("sbuf", [128, C], U8),
    "qp": ("sbuf", [128, C], F8), "sp": ("sbuf", [128, C], U8),
    "l4": ("sbuf", [128, C], F8), "m4": ("sbuf", [128, C], U8),
    "l2": ("sbuf", [128, C], F8), "m2": ("sbuf", [128, C], U8),
    "lh": ("sbuf", [128, C + H], F8), "mh": ("sbuf", [128, C + H], U8),
    "ls": ("sbuf", [128, C], F8), "ms": ("sbuf", [128, C], U8),
    "pa": ("psum", [128, 2048], F32), "pb": ("psum", [128, 2048], F32),
}
SEMAPHORES = (["fill", "eye", "zero", "ldb", "lda0", "lda1", "qb", "qw", "qt", "qp", "sent", "stored", "tev", "tevs", "pev", "pevs", "yev",
               "r4", "r2", "rh", "rs"]
              + [n + str(i) for n in ("qa", "mt", "mp", "my") for i in range(4)])


def rank_program(g, core, T, topo):
    rank = T.rank_of(core)
    if rank is None:
        return
    n = len(T.cores)
    at = lambda k: T.cores[(rank + k) % n]
    even = topo.rack(topo.host(core)) == topo.rack(topo.host(T.cores[0]))
    sem = T.sem
    v, s, t = g.vector, g.scalar, g.tensor
    copy = ActivationFunctionType.Copy
    u8 = T.sa.dtype
    total = [0]

    def engines(src, dst):
        return bin(topo.mask(src, dst)).count("1")

    def send(dst, codes, plane, src_codes, src_plane, rsem, to=(0, C), fr=(0, C)):
        rid, pid = topo.addr(dst, core)
        m = topo.mask(core, dst)
        g.remote_dma(codes[:, to[0]:to[1]].bitcast(u8), src_codes[:, fr[0]:fr[1]].bitcast(u8), sem[rsem], sem.sent, pid, rid, m)
        g.remote_dma(plane[:, to[0]:to[1]], src_plane[:, fr[0]:fr[1]], sem[rsem], sem.sent, pid, rid, m)
        total[0] += 2 * engines(core, dst)

    g.sync.dma_start(T.xb[:], T.b[:]).then_inc(sem.ldb, 16)
    s.dma_start(T.xa[:, 0:8 * C], T.a[:, 0:8 * C]).then_inc(sem.lda0, 16)
    g.sync.dma_start(T.xa[:, 8 * C:16 * C], T.a[:, 8 * C:16 * C]).then_inc(sem.lda1, 16)

    v.memset(T.eye[:], 0.0).then_inc(sem.fill, 1)
    g.wait_ge(sem.fill, 1)
    one = T.eye[:, 3:4 * C + 3:4]
    g.affine_select(one, one, [[-1, C]], AluOpType.not_equal, 1.0, 0, 1).then_inc(sem.eye, 1)
    land, zeros, view = ((0, H), (H, H + C), (0, C)) if even else ((C, C + H), (0, C), (H, H + C))
    v.wait_ge(sem.fill, 1)
    v.quantize_mx(T.lh[:, zeros[0]:zeros[1]], T.mh[:, zeros[0]:zeros[1]], T.eye[:, 4 * C + 4:8 * C + 4]).then_inc(sem.zero, 1)
    v.wait_ge(sem.eye, 1)
    for i in range(4):
        v.quantize_mx(T.qw[:, C * i:C * i + C], T.sw[:, C * i:C * i + C], T.eye[:, 3 - i:3 - i + 4 * C]).then_inc(sem.qw, 1)

    v.wait_ge(sem.ldb, 16)
    v.quantize_mx(T.qb[:], T.sb[:], T.xb[:]).then_inc(sem.qb, 1)
    for i in range(4):
        if i % 2 == 0:
            v.wait_ge(sem["lda%d" % (i // 2)], 16)
        v.quantize_mx(T.qa[:, C * i:C * i + C], T.sa[:, C * i:C * i + C], T.xa[:, 4 * C * i:4 * C * i + 4 * C]).then_inc(sem["qa%d" % i], 1)

    bank = lambda p, i: p[:, 512 * i:512 * i + C]

    def own(p, i, stop):
        return t.matmul_mx(bank(p, i), T.qa[:, C * i:C * i + C], T.sa[:, C * i:C * i + C], T.qb[:], T.sb[:], start=True, stop=stop)

    def unpack(p, i, codes, plane, stop, cols=(0, C)):
        return t.matmul_mx(bank(p, i), T.qw[:, C * i:C * i + C], T.sw[:, C * i:C * i + C],
                           codes[:, cols[0]:cols[1]], plane[:, cols[0]:cols[1]], start=False, stop=stop)

    t.wait_ge(sem.qb, 1)
    for i in range(4):
        t.wait_ge(sem["qa%d" % i], 1)
        own(T.pa, i, True).then_inc(sem["mt%d" % i], 1)
    for i in range(4):
        own(T.pb, i, False)
    t.wait_ge(sem.tev, 1)
    t.wait_ge(sem.tevs, 3)
    for i in range(4):
        own(T.pa, i, False)
    t.wait_ge(sem.qw, 4)
    t.wait_ge(sem.zero, 1)
    t.wait_ge(sem.r2, 2 * engines(at(-2), core))
    for p in (T.pb, T.pa):
        for i in range(4):
            unpack(p, i, T.l2, T.m2, False)
    if even:
        t.wait_ge(sem.r4, 2 * engines(at(-4), core))
        for i in range(4):
            unpack(T.pb, i, T.l4, T.m4, True).then_inc(sem["mp%d" % i], 1)
        for i in range(4):
            unpack(T.pa, i, T.l4, T.m4, False)
        t.wait_ge(sem.rh, 2 * engines(at(1), core))
        for i in range(4):
            unpack(T.pa, i, T.lh, T.mh, False, view)
        t.wait_ge(sem.rs, 2 * engines(at(-3), core))
    else:
        t.wait_ge(sem.rh, 2 * engines(at(2), core))
        for i in range(4):
            unpack(T.pb, i, T.lh, T.mh, True, view).then_inc(sem["mp%d" % i], 1)
        t.wait_ge(sem.r4, 2 * engines(at(-4), core))
        for i in range(4):
            unpack(T.pa, i, T.l4, T.m4, False)
        t.wait_ge(sem.rs, 2 * engines(at(-1), core))
    for i in range(4):
        unpack(T.pa, i, T.ls, T.ms, True).then_inc(sem["my%d" % i], 1)

    for i in (0, 1, 2):
        s.wait_ge(sem["mt%d" % i], 1)
        s.activation(T.tt[:, i:4 * C:4], bank(T.pa, i), copy).then_inc(sem.tevs, 1)
    for i in (0, 2):
        s.wait_ge(sem["mp%d" % i], 1)
        s.activation(T.pp[:, i:4 * C:4], bank(T.pb, i), copy).then_inc(sem.pevs, 1)
    for i in (0, 2):
        s.wait_ge(sem["my%d" % i], 1)
        s.activation(T.yt[:, i:4 * C:4], bank(T.pa, i), copy).then_inc(sem.yev, 1)
    v.wait_ge(sem.mt3, 1)
    v.tensor_copy(T.tt[:, 3:4 * C:4], bank(T.pa, 3)).then_inc(sem.tev, 1)
    v.wait_ge(sem.tevs, 3)
    v.wait_ge(sem.tev, 1)
    v.quantize_mx(T.qt[:], T.st[:], T.tt[:]).then_inc(sem.qt, 1)
    for i in (1, 3):
        v.wait_ge(sem["mp%d" % i], 1)
        v.tensor_copy(T.pp[:, i:4 * C:4], bank(T.pb, i)).then_inc(sem.pev, 1)
    v.wait_ge(sem.pevs, 2)
    v.wait_ge(sem.pev, 2)
    v.quantize_mx(T.qp[:], T.sp[:], T.pp[:]).then_inc(sem.qp, 1)
    for i in (1, 3):
        v.wait_ge(sem["my%d" % i], 1)
        v.tensor_copy(T.yt[:, i:4 * C:4], bank(T.pa, i)).then_inc(sem.yev, 1)
    g.sync.wait_ge(sem.yev, 4)
    g.sync.dma_start(T.y[:], T.yt[:]).then_inc(sem.stored, 16)
    g.sync.wait_ge(sem.stored, 16)

    g.wait_ge(sem.qt, 1)
    send(at(2), T.l2, T.m2, T.qt, T.st, "r2")
    if even:
        send(at(4), T.l4, T.m4, T.qt, T.st, "r4")
        g.wait_ge(sem.qp, 1)
        send(at(1), T.ls, T.ms, T.qp, T.sp, "rs")
    else:
        send(at(-2), T.lh, T.mh, T.qt, T.st, "rh", to=land, fr=(H, C))
        send(at(4), T.l4, T.m4, T.qt, T.st, "r4")
        g.wait_ge(sem.r2, 2 * engines(at(-2), core))
        send(at(-1), T.lh, T.mh, T.l2, T.m2, "rh", to=(0, H), fr=(0, H))
        g.wait_ge(sem.qp, 1)
        send(at(3), T.ls, T.ms, T.qp, T.sp, "rs")
    g.wait_ge(sem.sent, total[0])
